import numpy as np
import ml_dtypes


def mxq(x, axis, fmt="e4m3"):
    dtype, down = {"e4m3": (ml_dtypes.float8_e4m3fn, 7), "e5m2": (ml_dtypes.float8_e5m2, 14)}[fmt]
    v = np.moveaxis(np.asarray(x, np.float32).astype(ml_dtypes.bfloat16).astype(np.float64), axis, -1)
    blocks = v.reshape(v.shape[:-1] + (-1, 32))
    amax = np.abs(blocks).max(-1, keepdims=True)
    byte = np.maximum(np.where(amax > 0, np.frexp(amax)[1] - 1 + 127, 0) - down, 1)
    scale = np.exp2(byte - 127.0)
    codes = (blocks / scale).astype(np.float32).astype(dtype).astype(np.float64)
    return np.moveaxis((codes * scale).reshape(v.shape), -1, axis)


WIDE = False


def mx_kscale(k):
    if not WIDE:
        return np.ones(k)
    levels = np.array([30, -30])
    if k % 512:
        return np.exp2(np.random.permutation(np.resize(levels, k // 32))).repeat(32)
    a = np.empty((k // 512, 16))
    for p in range(k // 512):
        a[p, :8] = np.random.permutation(np.resize(levels, 8))
        for g in range(8):
            far = levels[np.abs(levels - a[p, g]) >= 10]
            a[p, g + 8] = far[np.random.randint(len(far))]
    return np.exp2(a.ravel()).repeat(32)


def f64(x):
    return np.asarray(x).astype(np.float64)


def striped(idx):
    return np.tile(np.asarray(idx).reshape(-1, 16).T, (8, 1)).astype(np.uint16)


def unstriped(offs):
    return offs[:16].T.reshape(-1).astype(np.int64)


E2M1 = np.array([0.0, 0.5, 1.0, 1.5, 2.0, 3.0, 4.0, 6.0, -0.0, -0.5, -1.0, -1.5, -2.0, -3.0, -4.0, -6.0])


def pack_weight(w, fmt):
    k, n = w.shape
    w = f64(np.asarray(w, np.float32).astype(ml_dtypes.bfloat16)).reshape(k // 32, 32, n)
    amax = np.abs(w).max(1)
    if fmt == "e4m3":
        byte = np.frexp(amax)[1] - 1 + 127 - 7
    else:
        mant, ex = np.frexp(amax / 6.0)
        byte = np.where(mant > 0.5, ex, ex - 1) + 127
    byte = np.clip(np.where(amax > 0, byte, 1), 1, 254)
    scaled = (w * np.exp2(127.0 - byte)[:, None, :]).reshape(k, n).astype(np.float32)
    by_word = np.ascontiguousarray(scaled.reshape(k // 512, 128, 4, n).transpose(0, 1, 3, 2))
    if fmt == "e4m3":
        words = by_word.astype(ml_dtypes.float8_e4m3fn).view(np.uint8)
    else:
        c = by_word.astype(ml_dtypes.float4_e2m1fn).view(np.uint8) & 0xF
        words = (c[..., 0::2] | (c[..., 1::2] << 4)).reshape(k // 512, 128, 2 * n)
    return np.ascontiguousarray(words), np.ascontiguousarray(byte.astype(np.uint8).reshape(k // 512, 16, n))


def unpack_weight(words, scales, fmt):
    g, _, n = scales.shape
    words = np.ascontiguousarray(words).reshape(g, 128, n, -1)
    if fmt == "e4m3":
        vals = words.view(ml_dtypes.float8_e4m3fn).astype(np.float64)
    else:
        nib = np.empty((g, 128, n, 4), np.uint8)
        nib[..., 0::2] = words & 0xF
        nib[..., 1::2] = words >> 4
        vals = E2M1[nib]
    vals = vals * np.repeat(np.exp2(scales.astype(np.float64) - 127.0), 8, axis=1)[..., None]
    return vals.transpose(0, 1, 3, 2).reshape(g * 512, n)


K, T, J, R, C, O, N, E = 512, 2048, 256, 512, 512, 256, 256, 1024


def setup_inputs():
    n = np.random.standard_normal
    idx = np.random.permutation(T)[:J]
    idx2 = np.random.permutation(T)[:J]
    idx3 = np.random.permutation(C)[:J]
    idx4 = np.random.permutation(C)[:J]
    idx5 = np.random.permutation(C)[:O]
    idx6 = np.random.permutation(E)[:O]
    fk = mx_kscale(K)
    fr = mx_kscale(R)
    xtp = pack_weight(n((K, T)) / fk[:, None], "e2m1")
    wp = pack_weight(n((K, R)) * 1 / np.sqrt(K) * fk[:, None] * fr, "e4m3")
    wbp = pack_weight(n((R, N)) * 1 / np.sqrt(R) / fr[:, None], "e2m1")
    return {
        "xt_words": xtp[0],
        "xt_scales": xtp[1],
        "w_words": wp[0],
        "w_scales": wp[1],
        "wb_words": wbp[0],
        "wb_scales": wbp[1],
        "offs": striped(idx),
        "offs2": striped(idx2),
        "offs3": striped(idx3),
        "offs4": striped(idx4),
        "offs5": striped(idx5),
        "offs6": striped(idx6),
    }


def reference(xt_words, xt_scales, w_words, w_scales, wb_words, wb_scales, offs, offs2, offs3, offs4, offs5, offs6):
    idx = unstriped(offs)
    idx2 = unstriped(offs2)
    idx3 = unstriped(offs3)
    idx4 = unstriped(offs4)
    idx5 = unstriped(offs5)
    idx6 = unstriped(offs6)
    xtu = unpack_weight(xt_words, xt_scales, "e2m1")
    wu = unpack_weight(w_words, w_scales, "e4m3")
    wbu = unpack_weight(wb_words, wb_scales, "e2m1")
    xtidxg = xtu[:, idx]
    a = wu.T @ xtidxg
    xtidx2g = xtu[:, idx2]
    b = wu.T @ xtidx2g
    pw = np.zeros((R, C))
    pw[:, idx3] = a
    pv = np.zeros((R, C))
    pv[:, idx4] = b
    pg = pw + pv
    hid = pg[:, idx5]
    hidq = mxq(hid, 0, "e5m2")
    p = wbu.T @ hidq
    y = np.zeros((N, E))
    y[:, idx6] = p
    return y

@@ -1,0 +1,178 @@
+from contextlib import ExitStack
+
+import concourse.mybir as mybir
+
+K, T, J, R, C, O, N, E = 512, 2048, 256, 512, 512, 256, 256, 1024
+FLOPS = 2 * K * R * 2 * J + 2 * R * N * O
+
+F32 = mybir.dt.float32
+BF16 = mybir.dt.bfloat16
+I32 = mybir.dt.int32
+U32 = mybir.dt.uint32
+U16 = mybir.dt.uint16
+U8 = mybir.dt.uint8
+E4M3X4 = mybir.dt.float8_e4m3fn_x4
+E5M2X4 = mybir.dt.float8_e5m2_x4
+E2M1X4 = mybir.dt.float4_e2m1fn_x4
+COPY = mybir.ActivationFunctionType.Copy
+
+P = 128
+PACK = 4
+
+
+def tile_list_tied_shared_one_scattered_kernel(
+    tc, xt_words, xt_scales, w_words, w_scales, wb_words, wb_scales,
+    offs, offs2, offs3, offs4, offs5, offs6, out,
+):
+    nc = tc.nc
+    with ExitStack() as ctx:
+        lists = ctx.enter_context(tc.tile_pool(name="lists", bufs=1))
+        sb = ctx.enter_context(tc.tile_pool(name="sb", bufs=1))
+        ps = ctx.enter_context(tc.psum_pool(name="ps", bufs=1))
+
+        def load_list(src, name):
+            t = lists.tile([P, J // 16], U16, name=name)
+            nc.sync.dma_start(t[:], src)
+            return t
+
+        def load_scales(dst, src):
+            for q in range(4):
+                nc.sync.dma_start(
+                    dst[32 * q : 32 * q + 4, :].bitcast(I32), src[0, 4 * q : 4 * q + 4, :].bitcast(I32)
+                )
+
+        x_scale = sb.tile([P, T], U8, name="x_scale", tag="x_scale_page", align_bytes=64)
+        w_scale_raw = sb.tile([P, R], U8, name="w_scale_raw", align_bytes=64)
+        wb_scale = sb.tile([P, N], U8, name="wb_scale", align_bytes=64)
+        nc.vector.memset(w_scale_raw[:].bitcast(I32), 0)
+        nc.vector.memset(x_scale[:].bitcast(I32), 0)
+
+        tok_a = load_list(offs, "tok_a")
+        tok_b = load_list(offs2, "tok_b")
+        load_scales(w_scale_raw, w_scales)
+        x_words = sb.tile([P, T], U16, name="x_words", align_bytes=64)
+        nc.sync.dma_start(x_words[:].bitcast(I32), xt_words[0].bitcast(I32))
+        w_raw = sb.tile([P, R], U32, name="w_raw", tag="w_raw_page", align_bytes=64)
+        nc.sync.dma_start(w_raw[:].bitcast(I32), w_words[0].rearrange("p r b -> p (r b)").bitcast(I32))
+        load_scales(x_scale, xt_scales)
+        col_a = load_list(offs3, "col_a")
+        col_b = load_list(offs4, "col_b")
+        nc.vector.memset(wb_scale[:].bitcast(I32), 0)
+        wb_codes = sb.tile([P, 2 * N], U8, name="wb_codes", align_bytes=64)
+        nc.sync.dma_start(wb_codes[:].bitcast(I32), wb_words[0].bitcast(I32))
+        load_scales(wb_scale, wb_scales)
+        col_read = load_list(offs5, "col_read")
+        col_out = load_list(offs6, "col_out")
+
+        board_a = [sb.tile([P, C], F32, name="board_a%d" % t) for t in range(PACK)]
+        board_b = [sb.tile([P, C], F32, name="board_b%d" % t) for t in range(PACK)]
+        for t in range(PACK):
+            nc.vector.memset(board_a[t][:], 0.0)
+            nc.vector.memset(board_b[t][:], 0.0)
+
+        w_codes = sb.tile([P, R], U32, name="w_codes", align_bytes=64)
+        nc.scalar.copy(
+            w_codes[:].rearrange("p (t m) -> p m t", t=PACK), w_raw[:].rearrange("p (m t) -> p m t", t=PACK)
+        )
+        w_scale = sb.tile([P, R], U8, name="w_scale", align_bytes=64)
+        nc.vector.tensor_copy(
+            w_scale[:].rearrange("p (t m) -> p t m", t=PACK), w_scale_raw[:].rearrange("p (m t) -> p t m", t=PACK)
+        )
+
+        picked = {}
+        for name, tok in (("a", tok_a), ("b", tok_b)):
+            words = sb.tile([P, J], U16, name="words_" + name, align_bytes=64)
+            scale = sb.tile([P, J], U8, name="scale_" + name, align_bytes=64)
+            nc.vector.tensor_copy(words[:], x_words[:].indirect(tok[:]))
+            nc.vector.tensor_copy(scale[:], x_scale[:].indirect(tok[:]))
+            picked[name] = (words, scale)
+
+        pages = [
+            sb.tile([P, E], F32, name="page0", tag="w_raw_page", align_bytes=64),
+            sb.tile([P, E], F32, name="page1", tag="x_scale_page", align_bytes=64),
+        ]
+        nc.gpsimd.memset(pages[0][:], 0.0)
+        nc.gpsimd.memset(pages[1][:], 0.0)
+
+        banks = {}
+        for half in range(2):
+            for name in ("a", "b"):
+                bank = ps.tile([P, 2, J], F32, name="bank_%s%d" % (name, half))
+                banks[name, half] = bank
+        for name in ("a", "b"):
+            words, scale = picked[name]
+            for t in range(PACK):
+                cols = slice(t * P, (t + 1) * P)
+                nc.tensor.matmul_mx(
+                    out=banks[name, t // 2][:, t % 2, :],
+                    lhsT=w_codes[:, cols].bitcast(E4M3X4), lhsT_scale=w_scale[:, cols],
+                    rhs=words[:].bitcast(E2M1X4), rhs_scale=scale[:],
+                    start=True, stop=True,
+                )
+
+        rows = {key: sb.tile([P, 2, J], F32, name="rows_%s%d" % key) for key in banks}
+        board = [sb.tile([P, C], F32, name="board%d" % t) for t in range(PACK)]
+        hid = sb.tile([P, O, PACK], BF16, name="hid", align_bytes=64)
+
+        def evac_s(key):
+            nc.scalar.copy(rows[key][:], banks[key][:])
+
+        def evac_v(key):
+            nc.vector.tensor_copy(rows[key][:], banks[key][:])
+
+        def put_s(dst, idx, src):
+            nc.scalar.activation(dst[:].indirect(idx[:]), src, COPY)
+
+        def put_v(dst, idx, src):
+            nc.vector.tensor_copy(dst[:].indirect(idx[:]), src)
+
+        def join(t):
+            nc.vector.tensor_tensor(board[t][:], board_a[t][:], board_b[t][:], mybir.AluOpType.add)
+
+        def look(t):
+            nc.vector.tensor_copy(hid[:, :, t], board[t][:].indirect(col_read[:]))
+
+        evac_s(("a", 0))
+        put_s(board_a[0], col_a, rows["a", 0][:, 0, :])
+        put_v(board_a[1], col_a, rows["a", 0][:, 1, :])
+        evac_v(("b", 0))
+        evac_s(("a", 1))
+        put_s(board_b[0], col_b, rows["b", 0][:, 0, :])
+        put_v(board_b[1], col_b, rows["b", 0][:, 1, :])
+        put_s(board_a[2], col_a, rows["a", 1][:, 0, :])
+        join(0)
+        join(1)
+        look(0)
+        look(1)
+        evac_s(("b", 1))
+        put_s(board_b[2], col_b, rows["b", 1][:, 0, :])
+        put_v(board_a[3], col_a, rows["a", 1][:, 1, :])
+        put_s(board_b[3], col_b, rows["b", 1][:, 1, :])
+        join(2)
+        look(2)
+        join(3)
+        look(3)
+
+        hid_codes = sb.tile([P, O], U32, name="hid_codes", align_bytes=64)
+        hid_scale = sb.tile([P, O], U8, name="hid_scale", align_bytes=64)
+        nc.vector.quantize_mx(
+            out=hid_codes[:].bitcast(E5M2X4), scales=hid_scale[:], in_=hid[:].rearrange("p o t -> p (o t)")
+        )
+        for h in range(2):
+            acc = ps.tile([P, O], F32, name="acc%d" % h)
+            nc.tensor.matmul_mx(
+                out=acc[:],
+                lhsT=wb_codes[:, 2 * P * h : 2 * P * (h + 1)].bitcast(E2M1X4),
+                lhsT_scale=wb_scale[:, P * h : P * (h + 1)],
+                rhs=hid_codes[:].bitcast(E5M2X4), rhs_scale=hid_scale[:],
+                start=True, stop=True,
+            )
+            res = sb.tile([P, O], F32, name="res%d" % h)
+            if h == 0:
+                nc.scalar.copy(res[:], acc[:])
+                put_s(pages[h], col_out, res[:])
+                nc.scalar.dma_start(out[P * h : P * (h + 1), :], pages[h][:])
+            else:
+                nc.vector.tensor_copy(res[:], acc[:])
+                put_v(pages[h], col_out, res[:])
+                nc.sync.dma_start(out[P * h : P * (h + 1), :], pages[h][:])

@@ -35,13 +35,13 @@ def tile_list_tied_shared_one_scattered_kernel(
             nc.sync.dma_start(t[:], src)
             return t
 
-        def load_scales(dst, src):
+        def load_scales(queue, dst, src):
             for q in range(4):
-                nc.sync.dma_start(
+                queue.dma_start(
                     dst[32 * q : 32 * q + 4, :].bitcast(I32), src[0, 4 * q : 4 * q + 4, :].bitcast(I32)
                 )
 
-        x_scale = sb.tile([P, T], U8, name="x_scale", tag="x_scale_page", align_bytes=64)
+        x_scale = sb.tile([P, T], U8, name="x_scale", align_bytes=64)
         w_scale_raw = sb.tile([P, R], U8, name="w_scale_raw", align_bytes=64)
         wb_scale = sb.tile([P, N], U8, name="wb_scale", align_bytes=64)
         nc.vector.memset(w_scale_raw[:].bitcast(I32), 0)
@@ -49,26 +49,28 @@ def tile_list_tied_shared_one_scattered_kernel(
 
         tok_a = load_list(offs, "tok_a")
         tok_b = load_list(offs2, "tok_b")
-        load_scales(w_scale_raw, w_scales)
+        load_scales(nc.scalar, w_scale_raw, w_scales)
         x_words = sb.tile([P, T], U16, name="x_words", align_bytes=64)
         nc.sync.dma_start(x_words[:].bitcast(I32), xt_words[0].bitcast(I32))
-        w_raw = sb.tile([P, R], U32, name="w_raw", tag="w_raw_page", align_bytes=64)
+        w_raw = sb.tile([P, R], U32, name="w_raw", align_bytes=64)
         nc.sync.dma_start(w_raw[:].bitcast(I32), w_words[0].rearrange("p r b -> p (r b)").bitcast(I32))
-        load_scales(x_scale, xt_scales)
+        load_scales(nc.sync, x_scale, xt_scales)
         col_a = load_list(offs3, "col_a")
         col_b = load_list(offs4, "col_b")
-        nc.vector.memset(wb_scale[:].bitcast(I32), 0)
-        wb_codes = sb.tile([P, 2 * N], U8, name="wb_codes", align_bytes=64)
-        nc.sync.dma_start(wb_codes[:].bitcast(I32), wb_words[0].bitcast(I32))
-        load_scales(wb_scale, wb_scales)
-        col_read = load_list(offs5, "col_read")
-        col_out = load_list(offs6, "col_out")
 
         board_a = [sb.tile([P, C], F32, name="board_a%d" % t) for t in range(PACK)]
         board_b = [sb.tile([P, C], F32, name="board_b%d" % t) for t in range(PACK)]
         for t in range(PACK):
-            nc.vector.memset(board_a[t][:], 0.0)
-            nc.vector.memset(board_b[t][:], 0.0)
+            nc.vector.memset(board_a[t][:].bitcast(I32), 0)
+        for t in range(PACK):
+            nc.vector.memset(board_b[t][:].bitcast(I32), 0)
+
+        nc.vector.memset(wb_scale[:].bitcast(I32), 0)
+        col_read = load_list(offs5, "col_read")
+        col_out = load_list(offs6, "col_out")
+        wb_codes = sb.tile([P, 2 * N], U8, name="wb_codes", align_bytes=64)
+        nc.sync.dma_start(wb_codes[:].bitcast(I32), wb_words[0].bitcast(I32))
+        load_scales(nc.sync, wb_scale, wb_scales)
 
         w_codes = sb.tile([P, R], U32, name="w_codes", align_bytes=64)
         nc.scalar.copy(
@@ -79,100 +81,120 @@ def tile_list_tied_shared_one_scattered_kernel(
             w_scale[:].rearrange("p (t m) -> p t m", t=PACK), w_scale_raw[:].rearrange("p (m t) -> p t m", t=PACK)
         )
 
-        picked = {}
+        words = {}
+        scale = {}
         for name, tok in (("a", tok_a), ("b", tok_b)):
-            words = sb.tile([P, J], U16, name="words_" + name, align_bytes=64)
-            scale = sb.tile([P, J], U8, name="scale_" + name, align_bytes=64)
-            nc.vector.tensor_copy(words[:], x_words[:].indirect(tok[:]))
-            nc.vector.tensor_copy(scale[:], x_scale[:].indirect(tok[:]))
-            picked[name] = (words, scale)
+            words[name] = sb.tile([P, J], U16, name="words_" + name, align_bytes=64)
+            nc.vector.tensor_copy(words[name][:], x_words[:].indirect(tok[:]))
+        for name, tok in (("a", tok_a), ("b", tok_b)):
+            scale[name] = sb.tile([P, J], U8, name="scale_" + name, align_bytes=64)
+            nc.vector.tensor_copy(scale[name][:], x_scale[:].indirect(tok[:]))
 
-        pages = [
-            sb.tile([P, E], F32, name="page0", tag="w_raw_page", align_bytes=64),
-            sb.tile([P, E], F32, name="page1", tag="x_scale_page", align_bytes=64),
-        ]
-        nc.gpsimd.memset(pages[0][:], 0.0)
-        nc.gpsimd.memset(pages[1][:], 0.0)
-
+        groups = [("a", (0,)), ("a", (1,)), ("a", (2, 3)), ("b", (0, 1)), ("b", (2, 3))]
         banks = {}
-        for half in range(2):
-            for name in ("a", "b"):
-                bank = ps.tile([P, 2, J], F32, name="bank_%s%d" % (name, half))
-                banks[name, half] = bank
-        for name in ("a", "b"):
-            words, scale = picked[name]
-            for t in range(PACK):
+        rows = {}
+        for name, slices in groups:
+            bank = ps.tile([P, len(slices), J], F32, name="bank_%s%d" % (name, slices[0]))
+            banks[name, slices[0]] = bank
+            for i, t in enumerate(slices):
                 cols = slice(t * P, (t + 1) * P)
                 nc.tensor.matmul_mx(
-                    out=banks[name, t // 2][:, t % 2, :],
+                    out=bank[:, i, :],
                     lhsT=w_codes[:, cols].bitcast(E4M3X4), lhsT_scale=w_scale[:, cols],
-                    rhs=words[:].bitcast(E2M1X4), rhs_scale=scale[:],
+                    rhs=words[name][:].bitcast(E2M1X4), rhs_scale=scale[name][:],
                     start=True, stop=True,
                 )
 
-        rows = {key: sb.tile([P, 2, J], F32, name="rows_%s%d" % key) for key in banks}
         board = [sb.tile([P, C], F32, name="board%d" % t) for t in range(PACK)]
-        hid = sb.tile([P, O, PACK], BF16, name="hid", align_bytes=64)
+        looked = sb.tile([P, PACK, O], BF16, name="looked", align_bytes=64)
+        lists_of = {"a": col_a, "b": col_b}
+        boards_of = {"a": board_a, "b": board_b}
 
-        def evac_s(key):
-            nc.scalar.copy(rows[key][:], banks[key][:])
+        def move(engine, dst, src):
+            if engine == "scalar":
+                nc.scalar.activation(dst, src, COPY)
+            else:
+                nc.vector.tensor_copy(dst, src)
 
-        def evac_v(key):
-            nc.vector.tensor_copy(rows[key][:], banks[key][:])
+        def evac(engine, name, first):
+            bank = banks[name, first]
+            tag = "stage_%s%d" % (name, first)
+            staged = sb.tile(bank.shape, F32, name=tag, tag=tag)
+            move(engine, staged[:], bank[:])
+            for i in range(bank.shape[1]):
+                rows[name, first + i] = staged[:, i, :]
 
-        def put_s(dst, idx, src):
-            nc.scalar.activation(dst[:].indirect(idx[:]), src, COPY)
+        def put(engine, name, t):
+            move(engine, boards_of[name][t][:].indirect(lists_of[name][:]), rows[name, t])
 
-        def put_v(dst, idx, src):
-            nc.vector.tensor_copy(dst[:].indirect(idx[:]), src)
+        def join(t, engine=nc.vector):
+            engine.tensor_tensor(board[t][:], board_a[t][:], board_b[t][:], mybir.AluOpType.add)
 
-        def join(t):
-            nc.vector.tensor_tensor(board[t][:], board_a[t][:], board_b[t][:], mybir.AluOpType.add)
+        def look(engine, t, lo, hi):
+            move(engine, looked[:, t, lo:hi], board[t][:].indirect(col_read[:, lo // 16 : hi // 16]))
 
-        def look(t):
-            nc.vector.tensor_copy(hid[:, :, t], board[t][:].indirect(col_read[:]))
+        def clear_page(h):
+            page = sb.tile([P, E], F32, name="page%d" % h, tag="stage_b%d" % (2 * h))
+            nc.gpsimd.memset(page[:], 0.0)
+            return page
 
-        evac_s(("a", 0))
-        put_s(board_a[0], col_a, rows["a", 0][:, 0, :])
-        put_v(board_a[1], col_a, rows["a", 0][:, 1, :])
-        evac_v(("b", 0))
-        evac_s(("a", 1))
-        put_s(board_b[0], col_b, rows["b", 0][:, 0, :])
-        put_v(board_b[1], col_b, rows["b", 0][:, 1, :])
-        put_s(board_a[2], col_a, rows["a", 1][:, 0, :])
+        evac("scalar", "a", 0)
+        evac("vector", "a", 1)
+        put("scalar", "a", 0)
+        put("vector", "a", 1)
+        evac("scalar", "a", 2)
+        evac("vector", "b", 0)
+        put("scalar", "a", 2)
+        put("vector", "b", 0)
+        put("scalar", "a", 3)
+        put("vector", "b", 1)
+        pages = [clear_page(0)]
+        evac("scalar", "b", 2)
         join(0)
         join(1)
-        look(0)
-        look(1)
-        evac_s(("b", 1))
-        put_s(board_b[2], col_b, rows["b", 1][:, 0, :])
-        put_v(board_a[3], col_a, rows["a", 1][:, 1, :])
-        put_s(board_b[3], col_b, rows["b", 1][:, 1, :])
+        put("scalar", "b", 2)
+        put("vector", "b", 3)
+        pages.append(clear_page(1))
+        look("scalar", 0, 0, O)
+        look("scalar", 1, 0, O)
         join(2)
-        look(2)
         join(3)
-        look(3)
+        look("scalar", 2, 0, O)
+        look("scalar", 3, 0, O // 2)
+        look("vector", 3, O // 2, O)
 
-        hid_codes = sb.tile([P, O], U32, name="hid_codes", align_bytes=64)
-        hid_scale = sb.tile([P, O], U8, name="hid_scale", align_bytes=64)
-        nc.vector.quantize_mx(
-            out=hid_codes[:].bitcast(E5M2X4), scales=hid_scale[:], in_=hid[:].rearrange("p o t -> p (o t)")
-        )
+        H = O // 2
+        woven = []
         for h in range(2):
-            acc = ps.tile([P, O], F32, name="acc%d" % h)
-            nc.tensor.matmul_mx(
-                out=acc[:],
-                lhsT=wb_codes[:, 2 * P * h : 2 * P * (h + 1)].bitcast(E2M1X4),
-                lhsT_scale=wb_scale[:, P * h : P * (h + 1)],
-                rhs=hid_codes[:].bitcast(E5M2X4), rhs_scale=hid_scale[:],
-                start=True, stop=True,
+            hid = sb.tile([P, H, PACK], BF16, name="hid%d" % h, align_bytes=64)
+            nc.vector.tensor_copy(
+                hid[:].rearrange("p (c i) t -> p c t i", i=4),
+                looked[:, :, h * H : (h + 1) * H].rearrange("p t (c i) -> p c t i", i=4),
             )
-            res = sb.tile([P, O], F32, name="res%d" % h)
-            if h == 0:
-                nc.scalar.copy(res[:], acc[:])
-                put_s(pages[h], col_out, res[:])
-                nc.scalar.dma_start(out[P * h : P * (h + 1), :], pages[h][:])
-            else:
-                nc.vector.tensor_copy(res[:], acc[:])
-                put_v(pages[h], col_out, res[:])
-                nc.sync.dma_start(out[P * h : P * (h + 1), :], pages[h][:])
+            woven.append(hid)
+        acc0 = [ps.tile([P, H], F32, name="acc0_%d" % h) for h in range(2)]
+        acc1 = ps.tile([P, O], F32, name="acc1")
+        for h in range(2):
+            hid_codes = sb.tile([P, H], U32, name="hid_codes%d" % h, align_bytes=64)
+            hid_scale = sb.tile([P, H], U8, name="hid_scale%d" % h, align_bytes=64)
+            nc.vector.quantize_mx(
+                out=hid_codes[:].bitcast(E5M2X4), scales=hid_scale[:], in_=woven[h][:].rearrange("p o t -> p (o t)")
+            )
+            for n, acc in ((0, acc0[h][:]), (1, acc1[:, h * H : (h + 1) * H])):
+                nc.tensor.matmul_mx(
+                    out=acc,
+                    lhsT=wb_codes[:, 2 * P * n : 2 * P * (n + 1)].bitcast(E2M1X4),
+                    lhsT_scale=wb_scale[:, P * n : P * (n + 1)],
+                    rhs=hid_codes[:].bitcast(E5M2X4), rhs_scale=hid_scale[:],
+                    start=True, stop=True,
+                )
+        res0 = [sb.tile([P, H], F32, name="res0_%d" % h) for h in range(2)]
+        res1 = sb.tile([P, O], F32, name="res1")
+        move("scalar", res0[0][:], acc0[0][:])
+        move("vector", res0[1][:], acc0[1][:])
+        move("vector", res1[:], acc1[:])
+        for h in range(2):
+            move("scalar", pages[0][:].indirect(col_out[:, h * H // 16 : (h + 1) * H // 16]), res0[h][:])
+        nc.scalar.dma_start(out[0:P, :], pages[0][:])
+        move("vector", pages[1][:].indirect(col_out[:]), res1[:])
+        nc.sync.dma_start(out[P : 2 * P, :], pages[1][:])

@@ -18,6 +18,10 @@ COPY = mybir.ActivationFunctionType.Copy
 
 P = 128
 PACK = 4
+QUADRANT = 32
+PER_COLUMN = 16
+HALF = O // 2
+MX_ALIGN = 64
 
 
 def tile_list_tied_shared_one_scattered_kernel(
@@ -30,85 +34,89 @@ def tile_list_tied_shared_one_scattered_kernel(
         sb = ctx.enter_context(tc.tile_pool(name="sb", bufs=1))
         ps = ctx.enter_context(tc.psum_pool(name="ps", bufs=1))
 
-        def load_list(src, name):
-            t = lists.tile([P, J // 16], U16, name=name)
-            nc.sync.dma_start(t[:], src)
-            return t
+        def load_list(src, tile_name):
+            offsets = lists.tile([P, J // PER_COLUMN], U16, name=tile_name)
+            nc.sync.dma_start(offsets[:], src)
+            return offsets
 
         def load_scales(queue, dst, src):
-            for q in range(4):
+            for u in range(P // QUADRANT):
                 queue.dma_start(
-                    dst[32 * q : 32 * q + 4, :].bitcast(I32), src[0, 4 * q : 4 * q + 4, :].bitcast(I32)
+                    dst[QUADRANT * u : QUADRANT * u + 4, :].bitcast(I32),
+                    src[0, 4 * u : 4 * u + 4, :].bitcast(I32),
                 )
 
-        x_scale = sb.tile([P, T], U8, name="x_scale", align_bytes=64)
-        w_scale_raw = sb.tile([P, R], U8, name="w_scale_raw", align_bytes=64)
-        wb_scale = sb.tile([P, N], U8, name="wb_scale", align_bytes=64)
+        x_scale = sb.tile([P, T], U8, name="x_scale", tag="x_scale", align_bytes=MX_ALIGN)
+        w_scale_raw = sb.tile([P, R], U8, name="w_scale_raw", tag="w_scale_raw", align_bytes=MX_ALIGN)
+        wb_scale = sb.tile([P, N], U8, name="wb_scale", align_bytes=MX_ALIGN)
         nc.vector.memset(w_scale_raw[:].bitcast(I32), 0)
         nc.vector.memset(x_scale[:].bitcast(I32), 0)
 
         tok_a = load_list(offs, "tok_a")
         tok_b = load_list(offs2, "tok_b")
         load_scales(nc.scalar, w_scale_raw, w_scales)
-        x_words = sb.tile([P, T], U16, name="x_words", align_bytes=64)
+        x_words = sb.tile([P, T], U16, name="x_words", tag="x_words", align_bytes=MX_ALIGN)
         nc.sync.dma_start(x_words[:].bitcast(I32), xt_words[0].bitcast(I32))
-        w_raw = sb.tile([P, R], U32, name="w_raw", align_bytes=64)
+        w_raw = sb.tile([P, R], U32, name="w_raw", tag="w_raw", align_bytes=MX_ALIGN)
         nc.sync.dma_start(w_raw[:].bitcast(I32), w_words[0].rearrange("p r b -> p (r b)").bitcast(I32))
         load_scales(nc.sync, x_scale, xt_scales)
         col_a = load_list(offs3, "col_a")
         col_b = load_list(offs4, "col_b")
 
         board_a = [sb.tile([P, C], F32, name="board_a%d" % t) for t in range(PACK)]
-        board_b = [sb.tile([P, C], F32, name="board_b%d" % t) for t in range(PACK)]
         for t in range(PACK):
             nc.vector.memset(board_a[t][:].bitcast(I32), 0)
-        for t in range(PACK):
-            nc.vector.memset(board_b[t][:].bitcast(I32), 0)
 
         nc.vector.memset(wb_scale[:].bitcast(I32), 0)
         col_read = load_list(offs5, "col_read")
         col_out = load_list(offs6, "col_out")
-        wb_codes = sb.tile([P, 2 * N], U8, name="wb_codes", align_bytes=64)
+        wb_codes = sb.tile([P, 2 * N], U8, name="wb_codes", align_bytes=MX_ALIGN)
         nc.sync.dma_start(wb_codes[:].bitcast(I32), wb_words[0].bitcast(I32))
         load_scales(nc.sync, wb_scale, wb_scales)
 
-        w_codes = sb.tile([P, R], U32, name="w_codes", align_bytes=64)
+        w_codes = sb.tile([P, R], U32, name="w_codes", align_bytes=MX_ALIGN)
         nc.scalar.copy(
             w_codes[:].rearrange("p (t m) -> p m t", t=PACK), w_raw[:].rearrange("p (m t) -> p m t", t=PACK)
         )
-        w_scale = sb.tile([P, R], U8, name="w_scale", align_bytes=64)
+        w_scale = sb.tile([P, R], U8, name="w_scale", align_bytes=MX_ALIGN)
         nc.vector.tensor_copy(
             w_scale[:].rearrange("p (t m) -> p t m", t=PACK), w_scale_raw[:].rearrange("p (m t) -> p t m", t=PACK)
         )
 
-        words = {}
-        scale = {}
-        for name, tok in (("a", tok_a), ("b", tok_b)):
-            words[name] = sb.tile([P, J], U16, name="words_" + name, align_bytes=64)
-            nc.vector.tensor_copy(words[name][:], x_words[:].indirect(tok[:]))
-        for name, tok in (("a", tok_a), ("b", tok_b)):
-            scale[name] = sb.tile([P, J], U8, name="scale_" + name, align_bytes=64)
-            nc.vector.tensor_copy(scale[name][:], x_scale[:].indirect(tok[:]))
+        picked_words = {}
+        picked_scale = {}
+        for side, tok in (("a", tok_a), ("b", tok_b)):
+            picked_words[side] = sb.tile([P, J], U16, name="words_" + side, align_bytes=MX_ALIGN)
+            nc.vector.tensor_copy(picked_words[side][:], x_words[:].indirect(tok[:]))
+        for side, tok in (("a", tok_a), ("b", tok_b)):
+            picked_scale[side] = sb.tile([P, J], U8, name="scale_" + side, align_bytes=MX_ALIGN)
+            nc.vector.tensor_copy(picked_scale[side][:], x_scale[:].indirect(tok[:]))
+
+        board_b = []
+        for t, freed in enumerate(("w_scale_raw", "w_raw", "x_words", "x_scale")):
+            cleared = sb.tile([P, C], F32, name="board_b%d" % t, tag=freed, align_bytes=MX_ALIGN)
+            nc.gpsimd.memset(cleared[:], 0.0)
+            board_b.append(cleared)
 
         groups = [("a", (0,)), ("a", (1,)), ("a", (2, 3)), ("b", (0, 1)), ("b", (2, 3))]
         banks = {}
-        rows = {}
-        for name, slices in groups:
-            bank = ps.tile([P, len(slices), J], F32, name="bank_%s%d" % (name, slices[0]))
-            banks[name, slices[0]] = bank
+        for side, slices in groups:
+            bank = ps.tile([P, len(slices), J], F32, name="bank_%s%d" % (side, slices[0]))
+            banks[side, slices[0]] = bank
             for i, t in enumerate(slices):
                 cols = slice(t * P, (t + 1) * P)
                 nc.tensor.matmul_mx(
                     out=bank[:, i, :],
                     lhsT=w_codes[:, cols].bitcast(E4M3X4), lhsT_scale=w_scale[:, cols],
-                    rhs=words[name][:].bitcast(E2M1X4), rhs_scale=scale[name][:],
+                    rhs=picked_words[side][:].bitcast(E2M1X4), rhs_scale=picked_scale[side][:],
                     start=True, stop=True,
                 )
 
         board = [sb.tile([P, C], F32, name="board%d" % t) for t in range(PACK)]
-        looked = sb.tile([P, PACK, O], BF16, name="looked", align_bytes=64)
-        lists_of = {"a": col_a, "b": col_b}
+        looked = sb.tile([P, PACK, O], BF16, name="looked", align_bytes=MX_ALIGN)
+        list_of = {"a": col_a, "b": col_b}
         boards_of = {"a": board_a, "b": board_b}
+        staged_slice = {}
 
         def move(engine, dst, src):
             if engine == "scalar":
@@ -116,85 +124,83 @@ def tile_list_tied_shared_one_scattered_kernel(
             else:
                 nc.vector.tensor_copy(dst, src)
 
-        def evac(engine, name, first):
-            bank = banks[name, first]
-            tag = "stage_%s%d" % (name, first)
+        def empty_bank(engine, side, first):
+            bank = banks[side, first]
+            tag = "stage_%s%d" % (side, first)
             staged = sb.tile(bank.shape, F32, name=tag, tag=tag)
             move(engine, staged[:], bank[:])
             for i in range(bank.shape[1]):
-                rows[name, first + i] = staged[:, i, :]
+                staged_slice[side, first + i] = staged[:, i, :]
 
-        def put(engine, name, t):
-            move(engine, boards_of[name][t][:].indirect(lists_of[name][:]), rows[name, t])
+        def put(engine, side, t):
+            move(engine, boards_of[side][t][:].indirect(list_of[side][:]), staged_slice[side, t])
 
-        def join(t, engine=nc.vector):
-            engine.tensor_tensor(board[t][:], board_a[t][:], board_b[t][:], mybir.AluOpType.add)
+        def join(t):
+            nc.vector.tensor_tensor(board[t][:], board_a[t][:], board_b[t][:], mybir.AluOpType.add)
 
         def look(engine, t, lo, hi):
-            move(engine, looked[:, t, lo:hi], board[t][:].indirect(col_read[:, lo // 16 : hi // 16]))
+            offsets = col_read[:, lo // PER_COLUMN : hi // PER_COLUMN]
+            move(engine, looked[:, t, lo:hi], board[t][:].indirect(offsets))
 
-        def clear_page(h):
-            page = sb.tile([P, E], F32, name="page%d" % h, tag="stage_b%d" % (2 * h))
+        def clear_page(n, freed):
+            page = sb.tile([P, E], F32, name="page%d" % n, tag=freed)
             nc.gpsimd.memset(page[:], 0.0)
             return page
 
-        evac("scalar", "a", 0)
-        evac("vector", "a", 1)
+        empty_bank("scalar", "a", 0)
+        empty_bank("vector", "a", 1)
         put("scalar", "a", 0)
         put("vector", "a", 1)
-        evac("scalar", "a", 2)
-        evac("vector", "b", 0)
+        empty_bank("scalar", "a", 2)
+        empty_bank("vector", "b", 0)
         put("scalar", "a", 2)
         put("vector", "b", 0)
         put("scalar", "a", 3)
         put("vector", "b", 1)
-        pages = [clear_page(0)]
-        evac("scalar", "b", 2)
+        pages = [clear_page(0, "stage_b0")]
+        empty_bank("scalar", "b", 2)
         join(0)
         join(1)
         put("scalar", "b", 2)
         put("vector", "b", 3)
-        pages.append(clear_page(1))
+        pages.append(clear_page(1, "stage_b2"))
         look("scalar", 0, 0, O)
         look("scalar", 1, 0, O)
         join(2)
         join(3)
         look("scalar", 2, 0, O)
-        look("scalar", 3, 0, O // 2)
-        look("vector", 3, O // 2, O)
+        look("scalar", 3, 0, HALF)
+        look("vector", 3, HALF, O)
 
-        H = O // 2
         woven = []
-        for h in range(2):
-            hid = sb.tile([P, H, PACK], BF16, name="hid%d" % h, align_bytes=64)
-            nc.vector.tensor_copy(
+        for half, weave in enumerate((nc.vector.tensor_copy, nc.scalar.copy)):
+            hid = sb.tile([P, HALF, PACK], BF16, name="hid%d" % half, align_bytes=MX_ALIGN)
+            weave(
                 hid[:].rearrange("p (c i) t -> p c t i", i=4),
-                looked[:, :, h * H : (h + 1) * H].rearrange("p t (c i) -> p c t i", i=4),
+                looked[:, :, half * HALF : (half + 1) * HALF].rearrange("p t (c i) -> p c t i", i=4),
             )
             woven.append(hid)
-        acc0 = [ps.tile([P, H], F32, name="acc0_%d" % h) for h in range(2)]
-        acc1 = ps.tile([P, O], F32, name="acc1")
-        for h in range(2):
-            hid_codes = sb.tile([P, H], U32, name="hid_codes%d" % h, align_bytes=64)
-            hid_scale = sb.tile([P, H], U8, name="hid_scale%d" % h, align_bytes=64)
+
+        sums = [ps.tile([P, O], F32, name="acc%d" % n) for n in range(N // P)]
+        for half in range(O // HALF):
+            hid_codes = sb.tile([P, HALF], U32, name="hid_codes%d" % half, align_bytes=MX_ALIGN)
+            hid_scale = sb.tile([P, HALF], U8, name="hid_scale%d" % half, align_bytes=MX_ALIGN)
             nc.vector.quantize_mx(
-                out=hid_codes[:].bitcast(E5M2X4), scales=hid_scale[:], in_=woven[h][:].rearrange("p o t -> p (o t)")
+                out=hid_codes[:].bitcast(E5M2X4), scales=hid_scale[:],
+                in_=woven[half][:].rearrange("p o t -> p (o t)"),
             )
-            for n, acc in ((0, acc0[h][:]), (1, acc1[:, h * H : (h + 1) * H])):
+            for n in range(N // P):
                 nc.tensor.matmul_mx(
-                    out=acc,
+                    out=sums[n][:, half * HALF : (half + 1) * HALF],
                     lhsT=wb_codes[:, 2 * P * n : 2 * P * (n + 1)].bitcast(E2M1X4),
                     lhsT_scale=wb_scale[:, P * n : P * (n + 1)],
                     rhs=hid_codes[:].bitcast(E5M2X4), rhs_scale=hid_scale[:],
                     start=True, stop=True,
                 )
-        res0 = [sb.tile([P, H], F32, name="res0_%d" % h) for h in range(2)]
-        res1 = sb.tile([P, O], F32, name="res1")
-        move("scalar", res0[0][:], acc0[0][:])
-        move("vector", res0[1][:], acc0[1][:])
-        move("vector", res1[:], acc1[:])
-        for h in range(2):
-            move("scalar", pages[0][:].indirect(col_out[:, h * H // 16 : (h + 1) * H // 16]), res0[h][:])
-        nc.scalar.dma_start(out[0:P, :], pages[0][:])
-        move("vector", pages[1][:].indirect(col_out[:]), res1[:])
-        nc.sync.dma_start(out[P : 2 * P, :], pages[1][:])
+
+        results = [sb.tile([P, O], F32, name="res%d" % n) for n in range(N // P)]
+        for n in range(N // P):
+            move("vector", results[n][:], sums[n][:])
+        for n, (engine, queue) in enumerate((("scalar", nc.scalar), ("vector", nc.sync))):
+            move(engine, pages[n][:].indirect(col_out[:]), results[n][:])
+            queue.dma_start(out[P * n : P * (n + 1), :], pages[n][:])

from contextlib import ExitStack

import concourse.mybir as mybir

K, T, J, R, C, O, N, E = 512, 2048, 256, 512, 512, 256, 256, 1024
FLOPS = 2 * K * R * 2 * J + 2 * R * N * O

F32 = mybir.dt.float32
BF16 = mybir.dt.bfloat16
I32 = mybir.dt.int32
U32 = mybir.dt.uint32
U16 = mybir.dt.uint16
U8 = mybir.dt.uint8
E4M3X4 = mybir.dt.float8_e4m3fn_x4
E5M2X4 = mybir.dt.float8_e5m2_x4
E2M1X4 = mybir.dt.float4_e2m1fn_x4
COPY = mybir.ActivationFunctionType.Copy

P = 128
PACK = 4
QUADRANT = 32
PER_COLUMN = 16
HALF = O // 2
MX_ALIGN = 64


def tile_list_tied_shared_one_scattered_kernel(
    tc, xt_words, xt_scales, w_words, w_scales, wb_words, wb_scales,
    offs, offs2, offs3, offs4, offs5, offs6, out,
):
    nc = tc.nc
    with ExitStack() as ctx:
        lists = ctx.enter_context(tc.tile_pool(name="lists", bufs=1))
        sb = ctx.enter_context(tc.tile_pool(name="sb", bufs=1))
        ps = ctx.enter_context(tc.psum_pool(name="ps", bufs=1))

        def load_list(src, tile_name):
            offsets = lists.tile([P, J // PER_COLUMN], U16, name=tile_name)
            nc.sync.dma_start(offsets[:], src)
            return offsets

        def load_scales(queue, dst, src):
            for u in range(P // QUADRANT):
                queue.dma_start(
                    dst[QUADRANT * u : QUADRANT * u + 4, :].bitcast(I32),
                    src[0, 4 * u : 4 * u + 4, :].bitcast(I32),
                )

        x_scale = sb.tile([P, T], U8, name="x_scale", tag="x_scale", align_bytes=MX_ALIGN)
        w_scale_raw = sb.tile([P, R], U8, name="w_scale_raw", tag="w_scale_raw", align_bytes=MX_ALIGN)
        wb_scale = sb.tile([P, N], U8, name="wb_scale", align_bytes=MX_ALIGN)
        nc.vector.memset(w_scale_raw[:].bitcast(I32), 0)
        nc.vector.memset(x_scale[:].bitcast(I32), 0)

        tok_a = load_list(offs, "tok_a")
        tok_b = load_list(offs2, "tok_b")
        load_scales(nc.scalar, w_scale_raw, w_scales)
        x_words = sb.tile([P, T], U16, name="x_words", tag="x_words", align_bytes=MX_ALIGN)
        nc.sync.dma_start(x_words[:].bitcast(I32), xt_words[0].bitcast(I32))
        w_raw = sb.tile([P, R], U32, name="w_raw", tag="w_raw", align_bytes=MX_ALIGN)
        nc.sync.dma_start(w_raw[:].bitcast(I32), w_words[0].rearrange("p r b -> p (r b)").bitcast(I32))
        load_scales(nc.sync, x_scale, xt_scales)
        col_a = load_list(offs3, "col_a")
        col_b = load_list(offs4, "col_b")

        board_a = [sb.tile([P, C], F32, name="board_a%d" % t) for t in range(PACK)]
        for t in range(PACK):
            nc.vector.memset(board_a[t][:].bitcast(I32), 0)

        nc.vector.memset(wb_scale[:].bitcast(I32), 0)
        col_read = load_list(offs5, "col_read")
        col_out = load_list(offs6, "col_out")
        wb_codes = sb.tile([P, 2 * N], U8, name="wb_codes", align_bytes=MX_ALIGN)
        nc.sync.dma_start(wb_codes[:].bitcast(I32), wb_words[0].bitcast(I32))
        load_scales(nc.sync, wb_scale, wb_scales)

        w_codes = sb.tile([P, R], U32, name="w_codes", align_bytes=MX_ALIGN)
        nc.scalar.copy(
            w_codes[:].rearrange("p (t m) -> p m t", t=PACK), w_raw[:].rearrange("p (m t) -> p m t", t=PACK)
        )
        w_scale = sb.tile([P, R], U8, name="w_scale", align_bytes=MX_ALIGN)
        nc.vector.tensor_copy(
            w_scale[:].rearrange("p (t m) -> p t m", t=PACK), w_scale_raw[:].rearrange("p (m t) -> p t m", t=PACK)
        )

        picked_words = {}
        picked_scale = {}
        for side, tok in (("a", tok_a), ("b", tok_b)):
            picked_words[side] = sb.tile([P, J], U16, name="words_" + side, align_bytes=MX_ALIGN)
            nc.vector.tensor_copy(picked_words[side][:], x_words[:].indirect(tok[:]))
        for side, tok in (("a", tok_a), ("b", tok_b)):
            picked_scale[side] = sb.tile([P, J], U8, name="scale_" + side, align_bytes=MX_ALIGN)
            nc.vector.tensor_copy(picked_scale[side][:], x_scale[:].indirect(tok[:]))

        board_b = []
        for t, freed in enumerate(("w_scale_raw", "w_raw", "x_words", "x_scale")):
            cleared = sb.tile([P, C], F32, name="board_b%d" % t, tag=freed, align_bytes=MX_ALIGN)
            nc.gpsimd.memset(cleared[:], 0.0)
            board_b.append(cleared)

        groups = [("a", (0,)), ("a", (1,)), ("a", (2, 3)), ("b", (0, 1)), ("b", (2, 3))]
        banks = {}
        for side, slices in groups:
            bank = ps.tile([P, len(slices), J], F32, name="bank_%s%d" % (side, slices[0]))
            banks[side, slices[0]] = bank
            for i, t in enumerate(slices):
                cols = slice(t * P, (t + 1) * P)
                nc.tensor.matmul_mx(
                    out=bank[:, i, :],
                    lhsT=w_codes[:, cols].bitcast(E4M3X4), lhsT_scale=w_scale[:, cols],
                    rhs=picked_words[side][:].bitcast(E2M1X4), rhs_scale=picked_scale[side][:],
                    start=True, stop=True,
                )

        board = [sb.tile([P, C], F32, name="board%d" % t) for t in range(PACK)]
        looked = sb.tile([P, PACK, O], BF16, name="looked", align_bytes=MX_ALIGN)
        list_of = {"a": col_a, "b": col_b}
        boards_of = {"a": board_a, "b": board_b}
        staged_slice = {}

        def move(engine, dst, src):
            if engine == "scalar":
                nc.scalar.activation(dst, src, COPY)
            else:
                nc.vector.tensor_copy(dst, src)

        def empty_bank(engine, side, first):
            bank = banks[side, first]
            tag = "stage_%s%d" % (side, first)
            staged = sb.tile(bank.shape, F32, name=tag, tag=tag)
            move(engine, staged[:], bank[:])
            for i in range(bank.shape[1]):
                staged_slice[side, first + i] = staged[:, i, :]

        def put(engine, side, t):
            move(engine, boards_of[side][t][:].indirect(list_of[side][:]), staged_slice[side, t])

        def join(t):
            nc.vector.tensor_tensor(board[t][:], board_a[t][:], board_b[t][:], mybir.AluOpType.add)

        def look(engine, t, lo, hi):
            offsets = col_read[:, lo // PER_COLUMN : hi // PER_COLUMN]
            move(engine, looked[:, t, lo:hi], board[t][:].indirect(offsets))

        def clear_page(n, freed):
            page = sb.tile([P, E], F32, name="page%d" % n, tag=freed)
            nc.gpsimd.memset(page[:], 0.0)
            return page

        empty_bank("scalar", "a", 0)
        empty_bank("vector", "a", 1)
        put("scalar", "a", 0)
        put("vector", "a", 1)
        empty_bank("scalar", "a", 2)
        empty_bank("vector", "b", 0)
        put("scalar", "a", 2)
        put("vector", "b", 0)
        put("scalar", "a", 3)
        put("vector", "b", 1)
        pages = [clear_page(0, "stage_b0")]
        empty_bank("scalar", "b", 2)
        join(0)
        join(1)
        put("scalar", "b", 2)
        put("vector", "b", 3)
        pages.append(clear_page(1, "stage_b2"))
        look("scalar", 0, 0, O)
        look("scalar", 1, 0, O)
        join(2)
        join(3)
        look("scalar", 2, 0, O)
        look("scalar", 3, 0, HALF)
        look("vector", 3, HALF, O)

        woven = []
        for half, weave in enumerate((nc.vector.tensor_copy, nc.scalar.copy)):
            hid = sb.tile([P, HALF, PACK], BF16, name="hid%d" % half, align_bytes=MX_ALIGN)
            weave(
                hid[:].rearrange("p (c i) t -> p c t i", i=4),
                looked[:, :, half * HALF : (half + 1) * HALF].rearrange("p t (c i) -> p c t i", i=4),
            )
            woven.append(hid)

        sums = [ps.tile([P, O], F32, name="acc%d" % n) for n in range(N // P)]
        for half in range(O // HALF):
            hid_codes = sb.tile([P, HALF], U32, name="hid_codes%d" % half, align_bytes=MX_ALIGN)
            hid_scale = sb.tile([P, HALF], U8, name="hid_scale%d" % half, align_bytes=MX_ALIGN)
            nc.vector.quantize_mx(
                out=hid_codes[:].bitcast(E5M2X4), scales=hid_scale[:],
                in_=woven[half][:].rearrange("p o t -> p (o t)"),
            )
            for n in range(N // P):
                nc.tensor.matmul_mx(
                    out=sums[n][:, half * HALF : (half + 1) * HALF],
                    lhsT=wb_codes[:, 2 * P * n : 2 * P * (n + 1)].bitcast(E2M1X4),
                    lhsT_scale=wb_scale[:, P * n : P * (n + 1)],
                    rhs=hid_codes[:].bitcast(E5M2X4), rhs_scale=hid_scale[:],
                    start=True, stop=True,
                )

        results = [sb.tile([P, O], F32, name="res%d" % n) for n in range(N // P)]
        for n in range(N // P):
            move("vector", results[n][:], sums[n][:])
        for n, (engine, queue) in enumerate((("scalar", nc.scalar), ("vector", nc.sync))):
            move(engine, pages[n][:].indirect(col_out[:]), results[n][:])
            queue.dma_start(out[P * n : P * (n + 1), :], pages[n][:])
